import numpy as np, ml_dtypes
CORES = [1,5,17,21,33,37,49,53]
N = 8
import mx_ref
BF = ml_dtypes.bfloat16
def gcols(t, e):
    v = np.concatenate([t.reshape(8, 16, -1, 4), np.zeros((8, 16, 1, 4), BF)], axis=2)
    return np.ascontiguousarray(np.stack([v[g][:, e[g]] for g in range(8)])).reshape(128, -1)
def tile(rs):
    return np.stack(rs, axis=2).reshape(128, -1).astype(BF)
def pick(q, e):
    c = np.concatenate([q[0].reshape(128, -1, 4), np.zeros((128, 1, 4), np.uint8)], axis=1); s = np.concatenate([q[1], np.ones((16, 1), np.uint8)], axis=1)
    return (np.ascontiguousarray(c[:, e].reshape(128, -1)), np.ascontiguousarray(s[:, e]))
def join(*qs):
    return (np.concatenate([q[0] for q in qs], axis=1), np.concatenate([q[1] for q in qs], axis=1))
def put(q, e, v):
    c, s = q[0].reshape(128, -1, 4).copy(), q[1].copy(); c[:, e] = v[0].reshape(128, -1, 4); s[:, e] = v[1]
    return (c.reshape(128, -1), s)
def pk(c, s):
    return (np.ascontiguousarray(c), mx_ref.live(s))
def emit(q):
    return q[0], q[1]
def packed(v, rng):
    q = [mx_ref.quantize(np.ascontiguousarray(v[r])) for r in range(N)]
    return np.stack([a for a, b in q]), np.stack([mx_ref.plane(b, rng) for a, b in q])
def values_of_codes():
    e, c = np.zeros((128, 128, 4), np.float32), np.zeros((128, 2, 4), np.uint8)
    e[np.arange(128), np.arange(128), 0] = 1
    c[:127, :, 0] = np.arange(256).reshape(2, 128).T[:127]
    return mx_ref.matmul(mx_ref.quantize(e.reshape(128, 512).astype(BF)), (c.reshape(128, 8), np.full((16, 2), 127, np.uint8))).T.reshape(-1).astype(np.float64)
CODE_VALUE, SCALE_VALUE = values_of_codes(), 2.0 ** (np.arange(256) - 127.0)
def decode(q):
    return (CODE_VALUE[q[0]].reshape(16, 8, -1, 4) * SCALE_VALUE[q[1]][:, None, :, None] + 0.0).reshape(128, -1).astype(np.float32)
def f(rng, *shape):
    return mx_ref.flush((rng.standard_normal(shape, dtype=np.float32) * np.exp2(rng.integers(-2, 3, shape[:-1] + (1,)))).astype(BF))
def wide(rng, *shape, cols=0):
    v = rng.standard_normal(shape, dtype=np.float32) * np.exp2(rng.integers(-12, 13, shape)).astype(np.float32)
    if cols: v *= np.repeat(np.exp2(rng.integers(-cols, cols + 1, shape[:-2] + (1, shape[-1] // 4))) * (rng.random(shape[:-2] + (1, shape[-1] // 4)) > 0.0625), 4, axis=-1).astype(np.float32)
    return mx_ref.flush(v.astype(BF))
C, R = 512, 2
def order(p):
    return np.argsort(-(p[::16] + np.float32(0.0)), axis=1, kind="stable")
def clear(v):
    v = np.array(v)
    v[np.abs(v.astype(np.float32)) < np.float32(2.0 ** -16)] = 0
    return v
def numbers_of(rng):
    return {"x": clear(f(rng, N, 128, 4 * C)), "u": np.array(f(rng, N, 128, 512)), "v": np.array(f(rng, N, 128, 512))}
def weights(rng, w):
    c, p = packed(np.stack([w] * N), rng)
    return {"wc": c, "ws": p}
def aside(rng, k):
    w = np.array(f(rng, 128, 2048)).reshape(8, 16, 4, 8, 16, 4)
    w[:, :k] = 0
    w[:, :, :, :, 0] = 0
    w[:, :, :, :, 8:] = 0
    return weights(rng, w.reshape(128, 2048))
def signs(rng):
    return np.stack([rng.permutation(8) % 2 * 2.0 - 1.0 for r in range(N)])
def setup_inputs(rng):
    return {**numbers_of(rng), **weights(rng, f(rng, 128, 2048))}
def setup_inputs_ties(rng):
    d = numbers_of(rng)
    e = rng.permutation(N)
    x = d["x"].reshape(N, 8, 16, C, 4)
    for r in range(N):
        k = np.zeros(C, int) if r == e[0] else rng.permutation(C) % 3
        a = x[r][:, :8, :3].copy()
        a[:, :, 2] = 0
        x[r][:, :8] = a[:, :, k]
    x[e[1]] = 0
    u = d["u"].reshape(N, 8, 16, 128, 4)
    u[:, :, 8:, ::16] = 0
    w = np.array(f(rng, 128, 2048)).reshape(8, 16, 4, 8, 16, 4)
    w[:, 8:, :, :, :8] = 0
    return {"x": x.reshape(N, 128, 4 * C), "u": u.reshape(N, 128, 512), "v": d["v"], **weights(rng, w.reshape(128, 2048))}
def setup_inputs_near(rng):
    d = numbers_of(rng)
    x = d["x"].astype(np.float32).reshape(N, 8, 16, C, 4)
    s = (np.arange(C) // 2 + rng.integers(0, C // 2, (N, 8, 1))) % (C // 2)
    g = ((s[..., None] >> np.arange(8)) & 1) * np.exp2(np.arange(8) - 23.0)
    x[:, :, 0] = 0
    x[:, :, 0, :, 0] = signs(rng)[:, :, None]
    x[:, :, 8] = g[..., :4]
    x[:, :, 9] = g[..., 4:]
    x[:, :, 10:] = 0
    u = d["u"].reshape(N, 128, 128, 4)
    u[:, :, ::16] = 0
    k = np.where(rng.permutation(N) < N // 2, 2.0 ** -30, 1.0).astype(np.float32).astype(BF)
    for h in range(0, 128, 16):
        u[:, h, h, 0] = k
        u[:, h + 8:h + 10, h] = k[:, None, None]
    return {"x": x.reshape(N, 128, 4 * C).astype(BF), "u": u.reshape(N, 128, 512), "v": d["v"], **aside(rng, 0)}
def setup_inputs_huge(rng):
    d = numbers_of(rng)
    x = 2.0 ** 30 * (0.6 + 0.4 * rng.random((N, 128, C, 4)))
    c = np.stack([rng.permutation(C) % 2 * 2.0 - 1.0 for r in range(N)])
    c[rng.permutation(N) < N // 2] = 1
    x *= c[:, None, :, None]
    u = d["u"].reshape(N, 128, 128, 4)
    a = 2.0 ** 30 * (1 - 0.25 * rng.random((N, 128, 8, 4))) * signs(rng)[:, None, :, None]
    u[:, :, ::16] = a.astype(np.float32).astype(BF)
    w = np.zeros((128, 4, 128, 4), np.float32)
    i = np.arange(128)
    for b in range(4): w[i, b, i, b] = 16
    return {"x": x.astype(np.float32).reshape(N, 128, 4 * C).astype(BF), "u": u.reshape(N, 128, 512), "v": d["v"], **weights(rng, w.reshape(128, 2048).astype(BF))}
def setup_inputs_crowd(rng):
    d = numbers_of(rng)
    x = d["x"].astype(np.float32).reshape(N, 8, 16, C, 4)
    a, b = np.triu_indices(N, 1)
    k = rng.permutation(len(a))[(np.arange(C)[None, :] + np.arange(8)[:, None]) % len(a)]
    z = rng.integers(4, 8, (8, 8, C, 4)) * rng.choice([-1.0, 1.0], (8, 8, C, 4)) * 2.0 ** 26
    s = C - 1 - np.arange(C)
    digits = np.stack([s % 8, s // 8 % 8, s // 64, 0 * s], axis=1)
    for r in range(N):
        l = rng.integers(4, 8, (8, 8, C, 4)) * rng.choice([-1.0, 1.0], (8, 8, C, 4))
        l = np.where((a[k] == r)[:, None, :, None], z, np.where((b[k] == r)[:, None, :, None], -z, l))
        for g in range(8):
            o = rng.permutation(C)
            p = x[r, g]
            p[8:, o] = l[g]
            p[0, o] = digits
    u = d["u"].reshape(N, 128, 128, 4)
    u[:, :, ::16] = 0
    for h in range(0, 128, 16): u[:, h, h, :3] = np.array([1, 8, 64], np.float32).astype(BF)
    return {"x": x.reshape(N, 128, 4 * C).astype(BF), "u": u.reshape(N, 128, 512), "v": d["v"], **aside(rng, 8)}
def setup_inputs_spread(rng):
    d = setup_inputs(rng)
    d["x"] = clear(wide(rng, N, 128, 4 * C, cols=6))
    return d
def check_inputs(d):
    b = []
    for k in ("x", "u", "v"):
        a = np.abs(d[k].astype(np.float32))
        if not (np.isfinite(a).all() and ((a == 0) | (a >= 2.0 ** -30) & (a <= 2.0 ** 30)).all()): b.append("a value of " + k)
    if (d["wc"] != d["wc"][:1]).any(): b.append("wc differs between ranks")
    s = [mx_ref.live(p) for p in d["ws"]]
    if any((p != s[0]).any() for p in s): b.append("ws differs between ranks")
    if not (np.abs(decode(pk(d["wc"][0], d["ws"][0]))) <= 2.0 ** 30).all(): b.append("a number of W beyond 2**30")
    return b
def reference(x, u, v, wc, ws):
    w = pk(wc[0], ws[0])
    lay = [pick(w, np.arange(128 * b, 128 * b + 128)) for b in range(4)]
    qu = [mx_ref.quantize(u[r]) for r in range(N)]
    now = [x[r] for r in range(N)]
    for t in range(R):
        o = [order(mx_ref.matmul(qu[r], mx_ref.quantize(now[r]))) for r in range(N)]
        total = decode(mx_ref.quantize(gcols(now[0], o[0])))
        for r in range(1, N): total = total + decode(mx_ref.quantize(gcols(now[r], o[r])))
        m = mx_ref.quantize((total * np.float32(0.125)).astype(BF))
        h = mx_ref.quantize(tile([np.maximum(mx_ref.matmul(lay[b], m), np.float32(0.0)) * np.float32(0.0625) for b in range(4)]))
        back = decode(h).astype(BF)
        for r in range(N):
            i = np.argsort(o[r], axis=1)
            now[r] = ((now[r].astype(np.float32) + gcols(back, i).astype(np.float32)) * np.float32(0.5)).astype(BF)
    y, ol = np.zeros((N, 128, C), np.float32), np.zeros((N, 8, C), np.float32)
    oc, osc = np.zeros((N, 128, 4 * C), np.uint8), np.zeros((N, 16, C), np.uint8)
    for r in range(N):
        q = mx_ref.quantize(now[r])
        y[r] = mx_ref.matmul(mx_ref.quantize(v[r]), q)
        ol[r] = o[r]
        oc[r], osc[r] = emit(q)
    return {"y": y, "ol": ol, "oc": oc, "osc": osc}

import numpy as np
from concourse.bass import DstId, RemoteDMATransfer
from concourse.mybir import dt, AluOpType as A, ActivationFunctionType as F

R = 2
C = 512
BL = 64
NS = [512, 448, 384, 320, 256, 192, 128, 128]
CO = [sum(NS[:s]) for s in range(8)]
FC = sum(NS)
ROWS = [[-1, 31, 30, 29]] + [[32 - 4 * s - t for t in range(4)] for s in range(1, 8)]
MINE = [1]
BIG = 2.0 ** 94

E4, U8, BF, F32, I32, U16 = "float8_e4m3fn_x4", "uint8", "bfloat16", "float32", "int32", "uint16"
SCRATCH = {}


def _sb(n, ty, *names):
    for k in names: SCRATCH[k] = ("sbuf", [128, n], ty)


def _mx(n, *pairs):
    for a, b in pairs:
        _sb(n, E4, a)
        _sb(n, U8, b)


_sb(2048, BF, "x0", "x1", "x2", "st", "sh", "sn", "eb", "junk")
_sb(512, BF, "ut", "vt", "bt", "bt2", "eighth", "mt", "ht", "c0", "bm", "maskb", "rst", "hold", "hk0", "hk")
_sb(4 * NS[1], BF, "sg")
_sb(4 * FC, BF, "ft")
_sb(512, F32, "iot", "pr", "pm", "sc", "cum", "e1", "e2", "inv", "olt", "yt")
_sb(192, F32, "acb")
_sb(32, F32, "m0", "ac0", "rs", "a1", "a2", "a2s", "a3")
_sb(1, F32, "pi", "pi1", "p15", "scol", "isc", "isc4")
_sb(1, I32, "p0", "p1")
_sb(8, I32, "uo0")
_sb(8, U16, "uoff")
_sb(32, U16, "il", "l0", "l1", "l2", "l3")
_mx(128, ("uq", "us"), ("ur", "urs"), ("vq", "vsc"), ("bq", "bs"), ("mq", "ms"), ("hq0", "hs0"), ("hq1", "hs1"))
_mx(512, ("wq", "wsc"), ("eq", "es"), ("xq0", "xs0"), ("xq1", "xs1"), ("xq2", "xs2"), ("sq0", "ss0"), ("sq1", "ss1"), ("hl0", "hp0"), ("hl1", "hp1"))
_mx(640, ("lc0", "ls0"), ("lc1", "ls1"))
_mx(FC, ("fq", "fs"))
SCRATCH.update({"pp": ("psum", [128, 512], F32), "pc": ("psum", [128, 512], F32), "pe": ("psum", [128, 512], F32), "pa": ("psum", [128, 2048], F32)})
SEMAPHORES = ["vs", "ss", "ps", "gs", "lx", "lu", "lv", "lw", "lws", "lsem", "so", "sy"]
SEMAPHORES += ["sa%d_%d" % (t, r) for t in range(R) for r in range(8)] + ["%s%d" % (k, t) for t in range(R) for k in ("ha", "cs", "ch")]


def owners(T, topo):
    by = {}
    for r, c in enumerate(T.cores): by.setdefault(topo.chip(c), []).append(r)
    first, second = [], []
    for k, ch in enumerate(sorted(by)):
        first.append(by[ch][k % 2])
        second.append(by[ch][1 - k % 2])
    return first + second


def rank_program(g, core, T, topo):
    rank = T.rank_of(core)
    if rank is None: return
    sem = T.sem
    V, S, P, Y = g.vector, g.scalar, g.tensor, g.sync
    Q = {"g": g, "v": V, "s": S, "p": P, "y": Y}
    SEM = {"v": "vs", "s": "ss", "p": "ps", "g": "gs"}
    cnt = {"vs": 0, "ss": 0, "ps": 0, "gs": 0}
    seen = {q: {} for q in Q}

    def need(q, *deps):
        for d in deps:
            if seen[q].get(d[0], 0) < d[1]:
                Q[q].wait_ge(sem[d[0]], d[1])
                seen[q][d[0]] = d[1]

    def done(q, inst):
        k = SEM[q]
        inst.then_inc(sem[k], 1)
        cnt[k] += 1
        return (k, cnt[k])

    def v(inst): return done("v", inst)
    def s(inst): return done("s", inst)
    def p(inst): return done("p", inst)
    def gg(inst): return done("g", inst)

    Y.dma_start(T.x0[:], T.x[:, :]).then_inc(sem.lx, 16)
    S.dma_start(T.ut[:], T.u[:, :]).then_inc(sem.lu, 16)
    Y.dma_start(T.wq[:].bitcast(dt.uint8), T.wc[:, :]).then_inc(sem.lw, 16)
    Y.dma_start(T.wsc[:], T.ws[:, :]).then_inc(sem.lws, 16)
    Y.dma_start(T.vt[:], T.v[:, :]).then_inc(sem.lv, 16)

    small = {"allow_small_or_imprecise_dtypes": True}
    k_p = gg(g.iota(T.p0[:], [[0, 1]], 0, 1))
    k_uo = gg(g.iota(T.uo0[:], [[16, 8]], 0, 0))
    k_c = gg(g.iota(T.c0[:], [[0, 32], [1, 16]], 0, 0, **small))
    k_m = gg(g.iota(T.m0[:], [[16, 32]], 15, 0, **small))
    c_8 = v(V.memset(T.eighth[:], 0.125))
    need("g", c_8)
    k_b0 = gg(g.affine_select(T.bt2[:], T.eighth[:], [[-16, 8], [0, 64]], A.is_ge, 0.0, 0, 1))
    need("g", k_b0)
    k_b1 = gg(g.affine_select(T.bt[:], T.bt2[:], [[16, 8], [0, 64]], A.is_ge, 0.0, 15, -1))
    k_io = gg(g.iota(T.iot[:], [[1, 512]], 1, 0, **small))
    for b in range(4):
        k_eb = gg(g.affine_select(T.eb[:, 512 * b:512 * b + 512], T.eighth[:], [[-1, 512]], A.is_equal, 0.0, b, 4))
    z = []
    for i in range(8):
        w = 64 if i < 7 else 128
        z.append(v(V.memset(T.ft[:, 4 * (CO[i] + NS[i] - w):4 * (CO[i] + NS[i])], 0.0)))
    c_rs = v(V.memset(T.rs[:], 0.0))
    need("v", k_p)
    c_p = v(V.tensor_scalar(T.p1[:], T.p0[:], 15, None, A.bitwise_and))
    need("v", k_uo)
    c_uoff = v(V.tensor_copy(T.uoff[:], T.uo0[:]))
    need("v", c_p)
    c_pi = v(V.tensor_copy(T.pi[:], T.p1[:]))
    c_pi1 = v(V.tensor_scalar(T.pi1[:], T.p1[:], 1.0, None, A.add))
    c_p15 = v(V.tensor_scalar(T.p15[:], T.p1[:], 15.0, None, A.is_equal))
    need("v", k_c, c_pi)
    c_bm = v(V.tensor_scalar(T.bm[:], T.c0[:], T.pi[:], None, A.not_equal))
    need("s", c_bm)
    c_mask = s(S.activation(T.maskb[:], T.bm[:], F.Copy, scale=-2.0 * BIG, bias=BIG))
    c_hold = v(V.tensor_scalar(T.hold[:], T.c0[:], 1.0, None, A.min))
    need("s", c_hold)
    c_rst = s(S.activation(T.rst[:], T.hold[:], F.Copy, scale=2.0 * BIG, bias=-BIG))
    need("v", ("lu", 16))
    c_uq = v(V.quantize_mx(T.uq[:], T.us[:], T.ut[:]))
    need("v", c_uq, c_uoff)
    c_ur = v(V.tensor_copy(T.ur[:, 0:128].bitcast(dt.uint32), T.uq[:, 0:128].bitcast(dt.uint32).indirect(T.uoff[:, 0:8])))
    need("s", c_uq)
    c_urs = s(S.activation(T.urs[:, 0:128], T.us[:, 0:128].indirect(T.uoff[:, 0:8]), F.Copy))
    c_hk0 = v(V.tensor_scalar(T.hk0[:], T.c0[:], T.pi1[:], 1024.0, A.is_equal, A.mult))
    need("v", ("lx", 16))
    xq = v(V.quantize_mx(T.xq0[:], T.xs0[:], T.x0[:]))
    need("v", c_hk0)
    c_hk = v(V.tensor_tensor(T.hk[:], T.hk0[:], T.bm[:], A.max))
    c_sc = v(V.tensor_scalar(T.scol[:], T.p15[:], -127.875, 128.0, A.mult, A.add))
    c_isc = v(V.tensor_scalar(T.isc[:], T.p15[:], 8.0 - 2.0 ** -7, 2.0 ** -7, A.mult, A.add))
    c_isc4 = v(V.tensor_scalar(T.isc4[:], T.p15[:], 4.0 - 2.0 ** -8, 2.0 ** -8, A.mult, A.add))
    need("v", k_m)
    c_ac0 = v(V.tensor_scalar(T.ac0[:], T.m0[:], T.pi[:], None, A.subtract))

    ow = owners(T, topo)
    own = ow.index(rank)
    mate = [r for r in range(len(T.cores)) if r != rank and topo.chip(T.cores[r]) == topo.chip(core)]
    far = [r for r in range(len(T.cores)) if topo.chip(T.cores[r]) != topo.chip(core)]
    fe = topo.engines(core, T.cores[far[0]])
    pairs = [fe[2 * k:2 * k + 2] for k in range(4)]
    ne = [e for e in topo.engines(core, T.cores[mate[0]]) if e not in fe][:4]
    local = [0]

    def put(src, rs, dst, sm, es):
        ids = []
        for r in rs:
            rid, pid, _se = topo.addr(T.cores[r])
            ids.append(DstId(rid=rid, pnc=pid))
        local[0] += len(es)
        return RemoteDMATransfer(dst_ids=ids, dma_engine_mask=sum(1 << e for e in es), remote_sem=sem[sm], srcs=[src], dsts=[dst] * len(rs))

    TURN = [([0, 1, 2], [3, 0, 1]), ([3, 2, 0], [1, 2, 3])]

    def quantise_flags(i, d):
        need("v", d)
        a, b = CO[i], CO[i] + NS[i]
        return v(V.quantize_mx(T.fq[:, a:b], T.fs[:, a:b], T.ft[:, 4 * a:4 * b]))

    jd = []
    for t in range(R):
        X, XN = T["x%d" % t], T["x%d" % (t + 1)]
        XQ, XS = T["xq%d" % t], T["xs%d" % t]
        SQ, SS, LC, LS = T["sq%d" % t], T["ss%d" % t], T["lc%d" % t], T["ls%d" % t]
        HQ, HS, HL, HP = T["hq%d" % t], T["hs%d" % t], T["hl%d" % t], T["hp%d" % t]
        last = t == R - 1
        need("p", xq, c_ur, c_urs)
        d_p = p(P.matmul_mx(T.pp[:], T.ur[:], T.urs[:], XQ[:], XS[:], True, True))
        need("v", d_p, c_mask)
        d_pm = v(V.tensor_tensor(T.pm[:], T.pp[:], T.maskb[:], A.min))
        need("s", d_pm)
        d_pr = s(S.activation(T.pr[:], T.pp[:], F.Copy))
        need("v", d_pm, c_rst)
        d_sc = v(V.tensor_tensor_scan(T.sc[:], T.rst[:], T.pm[:], -BIG, A.min, A.max))
        need("s", d_sc, c_rs, z[-1], d_pr)
        own_q = {}
        for i in MINE:
            f0, sg = 4 * CO[i], []
            for j in range(5):
                if j < 4:
                    m = ROWS[i][j]
                    sg.append(s(S.activation(T.sg[:, NS[1] * j:NS[1] * j + 16 * m], T.pr[:, 0:16 * m], F.Sign, scale=-1.0, bias=T.sc[:, 16 * m + 15:16 * m + 16])))
                if j > 0:
                    m = ROWS[i][j - 1]
                    need("s", sg[j - 1])
                    own_q[i] = s(S.activation(T.ft[:, f0 + j - 1:f0 + 64 * m:4], T.sg[:, NS[1] * (j - 1):NS[1] * (j - 1) + 16 * m], F.Relu, accum_out=T.rs[:, m:m + 1]))
        need("v", d_sc, d_pr, *z)
        quant, waiting, last_s = {}, None, None
        todo = [i for i in range(8) if i not in MINE]
        for i in todo:
            f0 = 4 * CO[i]
            for j, m in enumerate(ROWS[i]):
                if m < 0:
                    d = d_dg = v(V.tensor_tensor(T.ft[:, f0 + j:f0 + 4 * C:4], T.pp[:], T.sc[:], A.is_le))
                else:
                    d = v(V.tensor_scalar(T.ft[:, f0 + j:f0 + 64 * m:4], T.pp[:, 0:16 * m], T.sc[:, 16 * m + 15:16 * m + 16], None, A.is_lt))
                    jo = 512 * (len(jd) % 4)
                    need("s", d, *jd[-4:-3])
                    last_s = s(S.activation(T.junk[:, jo:jo + 16 * m], T.ft[:, f0 + j:f0 + 64 * m:4], F.Copy, accum_out=T.rs[:, m:m + 1]))
                    jd.append(last_s)
                if waiting is not None and j == 1:
                    quant[waiting[0]] = quantise_flags(*waiting)
                    waiting = None
                if i == todo[1] and j == 2:
                    if t == 0:
                        need("v", k_b1)
                        c_bq = v(V.quantize_mx(T.bq[:], T.bs[:], T.bt[:]))
                    need("v", d_dg, c_hold)
                    d_cum = v(V.tensor_tensor_scan(T.cum[:], T.hold[:], T.ft[:, 0:4 * C:4], 0.0, A.mult, A.add))
                if i == todo[3] and j == 2:
                    need("v", d_cum, c_ac0)
                    d_a1 = v(V.tensor_tensor(T.a1[:], T.ac0[:], T.cum[:, 15:512:16], A.subtract))
                    for k in MINE: quant[k] = quantise_flags(k, own_q[k])
            waiting = (i, d)
        quant[waiting[0]] = quantise_flags(*waiting)
        order = sorted(quant, key=lambda i: quant[i][1])
        for i in order:
            need("p", quant[i], c_bq)
            d_pc = p(P.matmul_mx(T.pc[:, 0:NS[i]], T.bq[:], T.bs[:], T.fq[:, CO[i]:CO[i] + NS[i]], T.fs[:, CO[i]:CO[i] + NS[i]], i == order[0], i == order[-1]))
        need("v", d_a1, last_s)
        d_a2 = v(V.tensor_tensor(T.a2[:], T.a1[:], T.rs[:], A.subtract))
        need("v", d_a2, c_sc)
        d_a2s = v(V.tensor_scalar(T.a2s[:], T.a2[:], T.scol[:], None, A.mult))
        need("v", d_pc, c_hk)
        d_e1 = v(V.tensor_tensor_scan(T.e1[:], T.hk[:], T.pc[:], 0.0, A.mult, A.max))
        need("v", d_e1, d_a2s)
        d_a3 = v(V.tensor_tensor(T.a3[:], T.e1[:, 15:512:16], T.a2s[:], A.add))
        need("v", d_a3, c_isc)
        d_il = v(V.tensor_scalar(T.il[:], T.a3[:], T.isc[:], None, A.mult))
        need("v", d_il, k_io)
        d_inv = v(V.tensor_copy(T.inv[:, 0:512].indirect(T.il[:, 0:32]), T.iot[:]))
        need("v", d_inv)
        d_e2 = v(V.tensor_tensor_scan(T.e2[:], T.hk[:], T.inv[:], 0.0, A.mult, A.max))
        need("v", d_e2, c_isc4)
        dl = {}
        for i in (2, 0, 3, 1):
            dl[i] = v(V.tensor_scalar(T["l%d" % i][:], T.e2[:, 15:512:16], T.isc4[:], float(i - 4), A.mult, A.add))
        for h in range(2):
            o = {}
            for i in (2, 3):
                need("s", dl[i])
                o[i] = s(S.activation(T.st[:, 1024 * h + i:1024 * h + 1024:4], X[:, 0:2048].indirect(T["l%d" % i][:, 16 * h:16 * h + 16]), F.Copy))
            for i in (0, 1):
                need("v", dl[i])
                o[i] = v(V.tensor_copy(T.st[:, 1024 * h + i:1024 * h + 1024:4], X[:, 0:2048].indirect(T["l%d" % i][:, 16 * h:16 * h + 16])))
            need("v", *o.values())
            d_q = v(V.quantize_mx(SQ[:, 256 * h:256 * h + 256], SS[:, 256 * h:256 * h + 256], T.st[:, 1024 * h:1024 * h + 1024]))
            need("g", d_q)
            blocks = [4 * h + k for k in range(4)]
            for kind in range(2):
                tr, k = [], 0
                for b in blocks:
                    r = ow[b]
                    if r == rank: continue
                    if r in mate: es = ne
                    else:
                        es = pairs[TURN[h][kind][k]]
                        k += 1
                    if kind == 0: sv, dv = SQ[:, BL * b:BL * b + BL].bitcast(dt.uint8), LC[:, BL * rank:BL * rank + BL].bitcast(dt.uint8)
                    else: sv, dv = SS[:, BL * b:BL * b + BL], LS[:, BL * rank:BL * rank + BL]
                    tr.append(put(sv, [r], dv, "sa%d_%d" % (t, rank), es))
                g.remote_dma_fused(tr, local_sem=sem.lsem)
            if own in blocks:
                need("y", d_q)
                Y.dma_start(LC[:, BL * rank:BL * rank + BL].bitcast(dt.uint8), SQ[:, BL * own:BL * own + BL].bitcast(dt.uint8)).then_inc(sem["cs%d" % t], 16)
                Y.dma_start(LS[:, BL * rank:BL * rank + BL], SS[:, BL * own:BL * own + BL]).then_inc(sem["cs%d" % t], 16)
        if t == 0:
            need("v", k_eb)
            c_eq = v(V.quantize_mx(T.eq[:], T.es[:], T.eb[:]))
            c_mt = v(V.memset(T.mt[:], 0.0))
            c_ht = v(V.memset(T.ht[:], 0.0))
            need("v", c_mt)
            for w in range(R): pad = v(V.quantize_mx(T["lc%d" % w][:, 512:640], T["ls%d" % w][:, 512:640], T.mt[:]))
        d_sh = v(V.tensor_scalar(T.sh[:], T.st[:], 0.125, None, A.mult))
        if last:
            d_ol = v(V.tensor_scalar(T.olt[:], T.inv[:], -1.0, None, A.add))
            need("v", ("lv", 16))
            c_vq = v(V.quantize_mx(T.vq[:], T.vsc[:], T.vt[:]))
        need("p", d_q, c_eq)
        arrived = lambda r: ("cs%d" % t, 32) if r == rank else ("sa%d_%d" % (t, r), 2 * len(ne) if r in mate else 4)
        E = lambda b: (T.eq[:, 128 * b:128 * b + 128], T.es[:, 128 * b:128 * b + 128])
        part = {(0, b): (T.pa, 512 * b) for b in (1, 2, 3)}
        part.update({(1, 1): (T.pp, 0), (1, 2): (T.pc, 0), (1, 3): (T.pe, 0)})

        def in_bank(r):
            if r == 7: need("p", pad)
            return p(P.matmul_mx(T.pa[:, 0:128], *E(0), LC[:, BL * r:BL * r + 128], LS[:, BL * r:BL * r + 128], r == 0, r == 7))

        d_u = {}
        for h in range(2):
            for r in range(4): need("p", arrived(4 * h + r))
            for b in (1, 2, 3):
                q, c = part[h, b]
                d_u[h, b] = p(P.matmul_mx(q[:, c:c + 256], *E(b), LC[:, 256 * h:256 * h + 256], LS[:, 256 * h:256 * h + 256], True, True))
            for r in ((0, 1, 2) if h == 0 else (3, 4, 5, 6, 7)): d_m0 = in_bank(r)
        acc = {}
        for b in (1, 2, 3):
            need("s", d_u[0, b])
            acc[b] = s(S.activation(T.acb[:, 64 * (b - 1):64 * b], T.pa[:, 512 * b:512 * b + 64], F.Copy))
        need("v", c_mt)
        for r in range(1, 8):
            for b in (1, 2, 3):
                q, c = part[r // 4, b]
                c += 64 * (r % 4)
                need("v", d_u[r // 4, b], acc[b])
                out = T.acb[:, 64 * (b - 1):64 * b] if r < 7 else T.mt[:, b:256:4]
                acc[b] = v(V.tensor_tensor(out, q[:, c:c + 64], T.acb[:, 64 * (b - 1):64 * b], A.add))
        need("s", d_m0, c_mt)
        d = s(S.activation(T.mt[:, 0:256:4], T.pa[:, 0:64], F.Copy))
        need("v", d, *acc.values())
        d_mq = v(V.quantize_mx(T.mq[:], T.ms[:], T.mt[:]))
        need("p", d_mq, ("lw", 16), ("lws", 16))
        d_h = [p(P.matmul_mx(T.pa[:, 512 * b:512 * b + 128], T.wq[:, 128 * b:128 * b + 128], T.wsc[:, 128 * b:128 * b + 128], T.mq[:], T.ms[:], True, True)) for b in range(4)]
        o = []
        for b in range(4):
            need("s" if b % 2 == 0 else "v", d_h[b], c_ht)
            if b % 2 == 0: o.append(s(S.activation(T.ht[:, b:256:4], T.pa[:, 512 * b:512 * b + 64], F.Relu, scale=0.0625)))
            else: o.append(v(V.tensor_scalar(T.ht[:, b:256:4], T.pa[:, 512 * b:512 * b + 64], 0.0, 0.0625, A.max, A.mult)))
        need("v", *o)
        d_hq = v(V.quantize_mx(HQ[:], HS[:], T.ht[:]))
        need("g", d_hq)
        for kind in range(2):
            if kind == 0: sv, dv = HQ[:, 0:BL].bitcast(dt.uint8), HL[:, BL * own:BL * own + BL].bitcast(dt.uint8)
            else: sv, dv = HS[:, 0:BL], HP[:, BL * own:BL * own + BL]
            g.remote_dma_fused([put(sv, far, dv, "ha%d" % t, fe), put(sv, mate, dv, "ha%d" % t, ne)], local_sem=sem.lsem)
        need("y", d_hq)
        Y.dma_start(HL[:, BL * own:BL * own + BL].bitcast(dt.uint8), HQ[:, 0:BL].bitcast(dt.uint8)).then_inc(sem["ch%d" % t], 16)
        Y.dma_start(HP[:, BL * own:BL * own + BL], HS[:, 0:BL]).then_inc(sem["ch%d" % t], 16)
        if last:
            need("y", d_ol)
            Y.dma_start(T.ol[:, :], T.olt[0:128:16, :]).then_inc(sem.so, 16)
        need("p", d_hq, ("ch%d" % t, 32), ("ha%d" % t, 2 * (len(far) * len(fe) + len(ne))))
        d_b = [p(P.matmul_mx(T.pa[:, 512 * b:512 * b + 512], *E(b), HL[:], HP[:], True, True)) for b in range(4)]
        o = []
        for b in range(4):
            need("v", d_b[b], d_sh)
            w = T.sn[:, 512 * b:512 * b + 512]
            d = v(V.tensor_tensor(w, T.pa[:, 512 * b:512 * b + 512], T.sh[:, b:2048:4], A.add))
            if b < 3:
                need("s", d)
                o.append(s(S.activation(XN[:, b:2048:4], w.indirect(T.il[:, 0:32]), F.Copy, scale=4.0)))
            else:
                need("v", d)
                o.append(v(V.tensor_scalar(XN[:, b:2048:4], w.indirect(T.il[:, 0:32]), 4.0, None, A.mult)))
        need("v", *o)
        xq = v(V.quantize_mx(T["xq%d" % (t + 1)][:], T["xs%d" % (t + 1)][:], XN[:]))

    XQ, XS = T["xq%d" % R], T["xs%d" % R]
    need("y", xq)
    Y.dma_start(T.oc[:, :], XQ[:].bitcast(dt.uint8)).then_inc(sem.so, 16)
    for k in range(4): Y.dma_start(T.osc[4 * k:4 * k + 4, :], XS[32 * k:32 * k + 4, :]).then_inc(sem.so, 16)
    need("p", xq, c_vq)
    d_y = [p(P.matmul_mx(b[:, 0:256], T.vq[:], T.vsc[:], XQ[:, 256 * k:256 * k + 256], XS[:, 256 * k:256 * k + 256], True, True)) for k, b in enumerate((T.pp, T.pc))]
    need("v", d_y[0])
    y0 = v(V.tensor_copy(T.yt[:, 0:256], T.pp[:, 0:256]))
    need("s", d_y[1])
    y1 = s(S.activation(T.yt[:, 256:512], T.pc[:, 0:256], F.Copy))
    need("y", y0)
    Y.dma_start(T.y[:, 0:256], T.yt[:, 0:256]).then_inc(sem.so, 16)
    need("s", y1)
    S.dma_start(T.y[:, 256:512], T.yt[:, 256:512]).then_inc(sem.sy, 16)
    need("s", ("sy", 16))
    need("y", *[(k, n) for k, n in cnt.items()], ("so", 16 * 7))
    need("g", ("lsem", local[0]))
